import numpy as np
import ml_dtypes


def mxq(x, axis, fmt="e4m3"):
    dtype, down = {"e4m3": (ml_dtypes.float8_e4m3fn, 7), "e5m2": (ml_dtypes.float8_e5m2, 14)}[fmt]
    v = np.moveaxis(np.asarray(x, np.float32).astype(ml_dtypes.bfloat16).astype(np.float64), axis, -1)
    blocks = v.reshape(v.shape[:-1] + (-1, 32))
    amax = np.abs(blocks).max(-1, keepdims=True)
    byte = np.maximum(np.where(amax > 0, np.frexp(amax)[1] - 1 + 127, 0) - down, 1)
    scale = np.exp2(byte - 127.0)
    codes = (blocks / scale).astype(np.float32).astype(dtype).astype(np.float64)
    return np.moveaxis((codes * scale).reshape(v.shape), -1, axis)


WIDE = False


def mx_kscale(k):
    if not WIDE:
        return np.ones(k)
    levels = np.array([10, -10, 5, -5, 0])
    if k % 512:
        return np.exp2(np.random.permutation(np.resize(levels, k // 32))).repeat(32)
    a = np.empty((k // 512, 16))
    for p in range(k // 512):
        a[p, :8] = np.random.permutation(np.resize(levels, 8))
        for g in range(8):
            far = levels[np.abs(levels - a[p, g]) >= 10]
            a[p, g + 8] = far[np.random.randint(len(far))]
    return np.exp2(a.ravel()).repeat(32)


def f64(x):
    return np.asarray(x).astype(np.float64)


def striped(idx):
    return np.tile(idx.reshape(-1, 16).T, (8, 1)).astype(np.uint16)


def unstriped(offs):
    return offs[:16].T.reshape(-1).astype(np.int64)


E2M1 = np.array([0.0, 0.5, 1.0, 1.5, 2.0, 3.0, 4.0, 6.0, -0.0, -0.5, -1.0, -1.5, -2.0, -3.0, -4.0, -6.0])


def pack_weight(w, fmt):
    k, n = w.shape
    w = f64(np.asarray(w, np.float32).astype(ml_dtypes.bfloat16)).reshape(k // 32, 32, n)
    amax = np.abs(w).max(1)
    if fmt == "e4m3":
        byte = np.frexp(amax)[1] - 1 + 127 - 7
    else:
        mant, ex = np.frexp(amax / 6.0)
        byte = np.where(mant > 0.5, ex, ex - 1) + 127
    byte = np.clip(np.where(amax > 0, byte, 1), 1, 254)
    scaled = (w * np.exp2(127.0 - byte)[:, None, :]).reshape(k, n).astype(np.float32)
    by_word = np.ascontiguousarray(scaled.reshape(k // 512, 128, 4, n).transpose(0, 1, 3, 2))
    if fmt == "e4m3":
        words = by_word.astype(ml_dtypes.float8_e4m3fn).view(np.uint8)
    else:
        c = by_word.astype(ml_dtypes.float4_e2m1fn).view(np.uint8) & 0xF
        words = (c[..., 0::2] | (c[..., 1::2] << 4)).reshape(k // 512, 128, 2 * n)
    return np.ascontiguousarray(words), np.ascontiguousarray(byte.astype(np.uint8).reshape(k // 512, 16, n))


def unpack_weight(words, scales, fmt):
    g, _, n = scales.shape
    words = np.ascontiguousarray(words).reshape(g, 128, n, -1)
    if fmt == "e4m3":
        vals = words.view(ml_dtypes.float8_e4m3fn).astype(np.float64)
    else:
        nib = np.empty((g, 128, n, 4), np.uint8)
        nib[..., 0::2] = words & 0xF
        nib[..., 1::2] = words >> 4
        vals = E2M1[nib]
    vals = vals * np.repeat(np.exp2(scales.astype(np.float64) - 127.0), 8, axis=1)[..., None]
    return vals.transpose(0, 1, 3, 2).reshape(g * 512, n)


def gelu(v):
    return 0.5 * v * (1.0 + np.tanh(np.sqrt(2.0 / np.pi) * (v + 0.044715 * v**3)))


K, T, S, H, P, N, P2 = 1536, 4096, 1024, 1024, 512, 768, 256

def setup_inputs():
    n = np.random.standard_normal
    sk = mx_kscale(K)[:, None]
    u = mx_kscale(H)[:, None]
    tab_words, tab_scales = pack_weight(n((K, T)) * sk, "e4m3")
    w4_words, w4_scales = pack_weight(n((H, N)) * 0.38 / np.sqrt(H) / u, "e2m1")
    return {
        "tab_words": tab_words,
        "tab_scales": tab_scales,
        "w1": (n((K, H)) * 1.3 / np.sqrt(K) / sk).astype(np.float32),
        "gain": (np.exp(0.3 * n(H)) * u[:, 0]).astype(np.float32),
        "inlet": np.exp(0.4 * n(H)).astype(np.float32),
        "w4_words": w4_words,
        "w4_scales": w4_scales,
        "offs": striped(np.random.permutation(T)[:S]),
        "pos1": striped(np.random.permutation(S)[:P]),
        "pos2": striped(np.random.permutation(S)[:P]),
        "pos3": striped(np.random.permutation(P)[:P2]),
        "pos4": striped(np.random.permutation(P)[:P2]),
    }

def reference(tab_words, tab_scales, w1, gain, inlet, w4_words, w4_scales, offs, pos1, pos2, pos3, pos4):
    v = unpack_weight(tab_words, tab_scales, "e4m3")[:, unstriped(offs)]
    x = mxq(f64(w1), 0, "e4m3").T @ v
    act = 0.5 * x * (1.0 + np.tanh(0.7978845608028654 * (x + 0.044715 * x ** 3)))
    h = act * f64(gain)[:, None]
    z = f64(inlet)[:, None] * h[:, unstriped(pos1)] - h[:, unstriped(pos2)]
    w4 = unpack_weight(w4_words, w4_scales, "e2m1")
    y = np.sin(w4.T @ mxq(z, 0, "e4m3"))
    return y[:, unstriped(pos3)] * y[:, unstriped(pos4)]

@@ -1,0 +1,252 @@
+from contextlib import ExitStack
+
+import concourse.mybir as mybir
+
+K, T, S, H, PAIRS, N, OUT_COLS = 1536, 4096, 1024, 1024, 512, 768, 256
+FLOPS = 2 * K * H * S + 2 * H * N * PAIRS
+
+F32 = mybir.dt.float32
+BF16 = mybir.dt.bfloat16
+I32 = mybir.dt.int32
+U32 = mybir.dt.uint32
+U16 = mybir.dt.uint16
+U8 = mybir.dt.uint8
+FP8X4 = mybir.dt.float8_e4m3fn_x4
+FP4X4 = mybir.dt.float4_e2m1fn_x4
+ACT = mybir.ActivationFunctionType
+ALU = mybir.AluOpType
+
+P = 128
+PACK = 4
+K_PASS = P * PACK
+K_PASSES = K // K_PASS
+H_PASSES = H // K_PASS
+BANK = 512
+N_TILES = N // P
+
+
+def tile_list_raceway_feeder_features_kernel(
+    tc, tab_words, tab_scales, w1, gain, inlet, w4_words, w4_scales, offs, pos1, pos2, pos3, pos4, out
+):
+    nc = tc.nc
+    with ExitStack() as ctx:
+        keep = ctx.enter_context(tc.tile_pool(name="keep", bufs=1))
+        psum = ctx.enter_context(tc.psum_pool(name="psum", bufs=1))
+
+        def load_list(dram, name):
+            tile = keep.tile(list(dram.shape), U16, name=name)
+            nc.sync.dma_start(tile[:], dram)
+            return tile
+
+        tab_sc = keep.tile([P, T], U8, name="tab_sc", align_bytes=64)
+        nc.vector.memset(tab_sc[:].bitcast(I32), 0)
+        w4_sc = keep.tile([P, H_PASSES, N], U8, name="w4_sc", align_bytes=64)
+        nc.vector.memset(w4_sc[:].rearrange("p a n -> p (a n)").bitcast(I32), 0)
+
+        inlet_sb = keep.tile([P, H_PASSES, PACK], F32, name="inlet_sb")
+        nc.scalar.dma_start(out=inlet_sb[:], in_=inlet.rearrange("(b p t) -> p b t", p=P, t=PACK))
+        gain_sb = keep.tile([P, H_PASSES, PACK], F32, name="gain_sb")
+        nc.scalar.dma_start(out=gain_sb[:], in_=gain.rearrange("(b p t) -> p b t", p=P, t=PACK))
+
+        def load_table(a):
+            tile = keep.tile([P, T], U32, name="tab%d" % a, align_bytes=64)
+            nc.sync.dma_start(out=tile[:].bitcast(I32), in_=tab_words[a].rearrange("p t i -> p (t i)").bitcast(I32))
+            return tile
+
+        def load_w1(b, a):
+            tile = keep.tile([P, PACK, K_PASS], F32, name="w1raw", tag="w1raw", bufs=4)
+            rows = w1[a * K_PASS : (a + 1) * K_PASS, b * K_PASS : (b + 1) * K_PASS]
+            nc.sync.dma_start(out=tile[:], in_=rows.rearrange("(p j) c -> p j c", j=PACK))
+            return tile
+
+        offs_sb = load_list(offs, "offs_sb")
+        pos1_sb = load_list(pos1, "pos1_sb")
+        pos2_sb = load_list(pos2, "pos2_sb")
+        pos3_sb = load_list(pos3, "pos3_sb")
+        pos4_sb = load_list(pos4, "pos4_sb")
+        tab = [load_table(0)]
+        for q in range(4):
+            nc.sync.dma_start(
+                out=tab_sc[32 * q : 32 * q + 4 * K_PASSES, :].bitcast(I32),
+                in_=tab_scales[:, 4 * q : 4 * q + 4, :].bitcast(I32),
+            )
+        tab.append(load_table(1))
+        tab.append(load_table(2))
+        raw = {}
+        for a in range(K_PASSES):
+            raw[0, a] = load_w1(0, a)
+        raw[1, 0] = load_w1(1, 0)
+
+        inlet_wide = keep.tile([P, H_PASSES * PACK, PAIRS], F32, name="inlet_wide")
+        nc.scalar.copy(
+            out=inlet_wide[:],
+            in_=inlet_sb[:].rearrange("p b t -> p (b t)").unsqueeze(2).to_broadcast([P, H_PASSES * PACK, PAIRS]),
+        )
+        neg_gain = keep.tile([P, H_PASSES, PACK], F32, name="neg_gain")
+        nc.vector.tensor_scalar(out=neg_gain[:], in0=gain_sb[:], scalar1=-1.0, scalar2=None, op0=ALU.mult)
+
+        v_codes = []
+        v_sc = keep.tile([P, S], U8, name="v_sc", align_bytes=64)
+        for a in range(K_PASSES):
+            codes = keep.tile([P, S], U32, name="v_codes%d" % a, align_bytes=64)
+            nc.vector.tensor_copy(out=codes[:], in_=tab[a][:].indirect(offs_sb[:]))
+            v_codes.append(codes)
+            if a == 0:
+                nc.vector.tensor_copy(out=v_sc[:], in_=tab_sc[:].indirect(offs_sb[:]))
+
+        grouped, w_codes, w_sc = {}, {}, {}
+
+        def round_w1(b, a, h, engine, tag):
+            tile = keep.tile([P, 2, P, PACK], BF16, name="w1bf", tag=tag, align_bytes=64)
+            dst = tile[:].rearrange("p t m j -> p m j t")
+            src = raw[b, a][:].rearrange("p j (m t) -> p m j t", t=PACK)[:, :, :, 2 * h : 2 * h + 2]
+            if engine == "vector":
+                nc.vector.tensor_copy(out=dst, in_=src)
+            else:
+                nc.scalar.copy(out=dst, in_=src)
+            grouped[b, a, h] = tile
+
+        def quantize_w1(b, a, h, tag):
+            codes = keep.tile([P, 2 * P], U32, name="w_codes", tag=tag, align_bytes=64)
+            scales = keep.tile([P, 2 * P], U8, name="w_sc%d%d%d" % (b, a, h), align_bytes=64)
+            nc.vector.quantize_mx(
+                out=codes[:].bitcast(FP8X4), scales=scales[:], in_=grouped[b, a, h][:].rearrange("p t m j -> p (t m j)")
+            )
+            w_codes[b, a, h], w_sc[b, a, h] = codes, scales
+
+        banks = {}
+
+        def first_product(b, t, a):
+            for s in range(S // BANK):
+                if a == 0:
+                    banks[b, t, s] = psum.tile([P, BANK], F32, name="bank", tag="bank%d" % (2 * t + s))
+                cols = slice(s * BANK, (s + 1) * BANK)
+                nc.tensor.matmul_mx(
+                    out=banks[b, t, s][:],
+                    lhsT=w_codes[b, a, t // 2][:, (t % 2) * P : (t % 2 + 1) * P].bitcast(FP8X4),
+                    lhsT_scale=w_sc[b, a, t // 2][:, (t % 2) * P : (t % 2 + 1) * P],
+                    rhs=v_codes[a][:, cols].bitcast(FP8X4),
+                    rhs_scale=v_sc[4 * a :, cols],
+                    start=(a == 0),
+                    stop=(a == K_PASSES - 1),
+                )
+
+        act = {}
+
+        def gelu(b, t):
+            tile = keep.tile([P, S], F32, name="act", tag="act", bufs=4)
+            for s in range(S // BANK):
+                nc.scalar.activation(out=tile[:, s * BANK : (s + 1) * BANK], in_=banks[b, t, s][:], func=ACT.Gelu_apprx_tanh)
+            act[b, t] = tile
+
+        diff = [keep.tile([P, PACK, PAIRS], F32, name="diff%d" % b) for b in range(H_PASSES)]
+
+        def pick_pairs(b, t, tag):
+            scaled = keep.tile([P, PAIRS], F32, name="scaled", tag=tag, align_bytes=64)
+            nc.vector.tensor_tensor(
+                out=scaled[:], in0=act[b, t][:].indirect(pos1_sb[:]), in1=inlet_wide[:, PACK * b + t, :], op=ALU.mult
+            )
+            nc.vector.tensor_tensor(
+                out=diff[b][:, t, :], in0=act[b, t][:].indirect(pos2_sb[:]), in1=scaled[:], op=ALU.subtract
+            )
+
+        for a in range(K_PASSES):
+            round_w1(0, a, 0, "vector", "bf0%d0" % a)
+            quantize_w1(0, a, 0, "codes0%d0" % a)
+            round_w1(0, a, 1, "scalar" if a < K_PASSES - 1 else "vector", "bf0%d1" % a)
+            quantize_w1(0, a, 1, "codes0%d1" % a)
+        raw[1, 1] = load_w1(1, 1)
+        raw[1, 2] = load_w1(1, 2)
+        w4_codes = keep.tile([P, H_PASSES, 2 * N], U8, name="w4_codes", align_bytes=64)
+        nc.sync.dma_start(out=w4_codes[:].bitcast(I32), in_=w4_words.rearrange("a p c -> p a c").bitcast(I32))
+        for q in range(4):
+            nc.sync.dma_start(
+                out=w4_sc[32 * q : 32 * q + 4, :, :].bitcast(I32),
+                in_=w4_scales[:, 4 * q : 4 * q + 4, :].rearrange("a r n -> r a n").bitcast(I32),
+            )
+
+        for a in range(K_PASSES):
+            for t in range(PACK):
+                first_product(0, t, a)
+        gelu(0, 0)
+        pick_pairs(0, 0, "scaled0")
+        gelu(0, 1)
+        pick_pairs(0, 1, "scaled1")
+        round_w1(1, 0, 0, "scalar", "codes020")
+        round_w1(1, 0, 1, "scalar", "codes021")
+        quantize_w1(1, 0, 0, "codes100")
+        quantize_w1(1, 0, 1, "codes101")
+        gelu(0, 2)
+        pick_pairs(0, 2, "codes021")
+        round_w1(1, 1, 0, "scalar", "codes020")
+        round_w1(1, 1, 1, "scalar", "scaled0")
+        quantize_w1(1, 1, 0, "codes110")
+        quantize_w1(1, 1, 1, "codes111")
+        round_w1(1, 2, 0, "vector", "codes020")
+        quantize_w1(1, 2, 0, "codes120")
+        gelu(0, 3)
+        pick_pairs(0, 3, "codes020")
+        round_w1(1, 2, 1, "scalar", "scaled1")
+        quantize_w1(1, 2, 1, "codes121")
+        for t in range(PACK):
+            for a in range(K_PASSES):
+                first_product(1, t, a)
+
+        z_bf = [keep.tile([P, PAIRS, PACK], BF16, name="z_bf%d" % b, align_bytes=64) for b in range(H_PASSES)]
+        z0 = keep.tile([P, PACK, PAIRS], F32, name="z0")
+        z_codes, z_sc = {}, {}
+
+        def apply_gain(t):
+            nc.scalar.activation(out=z0[:, t, :], in_=diff[0][:, t, :], func=ACT.Copy, scale=neg_gain[:, 0, t : t + 1])
+
+        def quantize_z(b):
+            codes = keep.tile([P, PAIRS], U32, name="z_codes%d" % b, align_bytes=64)
+            scales = keep.tile([P, PAIRS], U8, name="z_sc%d" % b, align_bytes=64)
+            nc.vector.quantize_mx(
+                out=codes[:].bitcast(FP8X4), scales=scales[:], in_=z_bf[b][:].rearrange("p m t -> p (m t)")
+            )
+            z_codes[b], z_sc[b] = codes, scales
+
+        gelu(1, 0)
+        pick_pairs(1, 0, "scaled0")
+        for t in range(PACK - 1):
+            apply_gain(t)
+        gelu(1, 1)
+        pick_pairs(1, 1, "scaled1")
+        apply_gain(PACK - 1)
+        gelu(1, 2)
+        pick_pairs(1, 2, "scaled0")
+        nc.scalar.copy(
+            out=z_bf[0][:].rearrange("p (c i) t -> p c t i", i=4),
+            in_=z0[:].rearrange("p t (c i) -> p c t i", i=4),
+        )
+        quantize_z(0)
+        gelu(1, 3)
+        pick_pairs(1, 3, "scaled1")
+        nc.vector.tensor_tensor(
+            out=z_bf[1][:].rearrange("p (c i) t -> p c t i", i=4),
+            in0=diff[1][:].rearrange("p t (c i) -> p c t i", i=4),
+            in1=neg_gain[:, 1, :].unsqueeze(1).unsqueeze(3).to_broadcast([P, PAIRS // 4, PACK, 4]),
+            op=ALU.mult,
+        )
+        quantize_z(1)
+
+        for i in range(N_TILES):
+            bank = psum.tile([P, BANK], F32, name="bank", tag="bank%d" % i)
+            for b in range(H_PASSES):
+                nc.tensor.matmul_mx(
+                    out=bank[:],
+                    lhsT=w4_codes[:, b, 2 * i * P : 2 * (i + 1) * P].bitcast(FP4X4),
+                    lhsT_scale=w4_sc[:, b, i * P : (i + 1) * P],
+                    rhs=z_codes[b][:].bitcast(FP8X4),
+                    rhs_scale=z_sc[b][:],
+                    start=(b == 0),
+                    stop=(b == H_PASSES - 1),
+                )
+            y = keep.tile([P, PAIRS], F32, name="y", tag="y", bufs=4)
+            nc.scalar.activation(out=y[:], in_=bank[:], func=ACT.Sin)
+            left = keep.tile([P, OUT_COLS], F32, name="left", tag="left", bufs=2)
+            nc.vector.tensor_copy(out=left[:], in_=y[:].indirect(pos3_sb[:]))
+            res = keep.tile([P, OUT_COLS], F32, name="res", tag="res", bufs=N_TILES)
+            nc.vector.tensor_tensor(out=res[:], in0=y[:].indirect(pos4_sb[:]), in1=left[:], op=ALU.mult)
+            nc.sync.dma_start(out=out[i * P : (i + 1) * P, :], in_=res[:])

@@ -23,6 +23,7 @@ K_PASSES = K // K_PASS
 H_PASSES = H // K_PASS
 BANK = 512
 N_TILES = N // P
+PARTS = ((0, 256), (256, 512), (512, 1024))
 
 
 def tile_list_raceway_feeder_features_kernel(
@@ -43,120 +44,61 @@ def tile_list_raceway_feeder_features_kernel(
         w4_sc = keep.tile([P, H_PASSES, N], U8, name="w4_sc", align_bytes=64)
         nc.vector.memset(w4_sc[:].rearrange("p a n -> p (a n)").bitcast(I32), 0)
 
-        inlet_sb = keep.tile([P, H_PASSES, PACK], F32, name="inlet_sb")
-        nc.scalar.dma_start(out=inlet_sb[:], in_=inlet.rearrange("(b p t) -> p b t", p=P, t=PACK))
-        gain_sb = keep.tile([P, H_PASSES, PACK], F32, name="gain_sb")
-        nc.scalar.dma_start(out=gain_sb[:], in_=gain.rearrange("(b p t) -> p b t", p=P, t=PACK))
+        def load_vector(dram, name):
+            tile = keep.tile([P, 4, PACK], F32, name=name)
+            for e in range(2):
+                nc.scalar.dma_start(out=tile[64 * e : 64 * (e + 1)], in_=dram.rearrange("(x m t) -> m x t", x=4, t=PACK))
+            return tile
+
+        def by_tile(raw_vec, factor, name):
+            tile = keep.tile([P, 8], F32, name=name)
+            for e in range(2):
+                rows = slice(64 * e, 64 * (e + 1))
+                nc.vector.tensor_scalar(
+                    out=tile[rows, 0:4].rearrange("p (u h) -> p u h", u=2),
+                    in0=raw_vec[rows, 0:2, e::2],
+                    scalar1=factor,
+                    scalar2=None,
+                    op0=ALU.mult,
+                )
+                nc.vector.tensor_scalar(
+                    out=tile[rows, 4:8], in0=raw_vec[rows, 2 + e, :], scalar1=factor, scalar2=None, op0=ALU.mult
+                )
+            return tile
 
         def load_table(a):
-            tile = keep.tile([P, T], U32, name="tab%d" % a, align_bytes=64)
+            tile = keep.tile([P, T], U32, name="tab", tag="tab%d" % a, align_bytes=64)
             nc.sync.dma_start(out=tile[:].bitcast(I32), in_=tab_words[a].rearrange("p t i -> p (t i)").bitcast(I32))
             return tile
 
-        def load_w1(b, a):
-            tile = keep.tile([P, PACK, K_PASS], F32, name="w1raw", tag="w1raw", bufs=4)
-            rows = w1[a * K_PASS : (a + 1) * K_PASS, b * K_PASS : (b + 1) * K_PASS]
-            nc.sync.dma_start(out=tile[:], in_=rows.rearrange("(p j) c -> p j c", j=PACK))
-            return tile
+        raw = {}
 
+        def load_w1(part, a):
+            c0, c1 = PARTS[part]
+            tile = keep.tile([P, PACK, c1 - c0], F32, name="w1raw%d%d" % (part, a))
+            rows = w1[a * K_PASS : (a + 1) * K_PASS, c0:c1]
+            nc.sync.dma_start(out=tile[:], in_=rows.rearrange("(p j) c -> p j c", j=PACK))
+            raw[part, a] = tile
+
+        inlet_raw = load_vector(inlet, "inlet_raw")
+        gain_raw = load_vector(gain, "gain_raw")
         offs_sb = load_list(offs, "offs_sb")
         pos1_sb = load_list(pos1, "pos1_sb")
         pos2_sb = load_list(pos2, "pos2_sb")
-        pos3_sb = load_list(pos3, "pos3_sb")
-        pos4_sb = load_list(pos4, "pos4_sb")
-        tab = [load_table(0)]
+        tab = {0: load_table(0)}
+        load_w1(0, 2)
         for q in range(4):
             nc.sync.dma_start(
                 out=tab_sc[32 * q : 32 * q + 4 * K_PASSES, :].bitcast(I32),
                 in_=tab_scales[:, 4 * q : 4 * q + 4, :].bitcast(I32),
             )
-        tab.append(load_table(1))
-        tab.append(load_table(2))
-        raw = {}
-        for a in range(K_PASSES):
-            raw[0, a] = load_w1(0, a)
-        raw[1, 0] = load_w1(1, 0)
-
-        inlet_wide = keep.tile([P, H_PASSES * PACK, PAIRS], F32, name="inlet_wide")
-        nc.scalar.copy(
-            out=inlet_wide[:],
-            in_=inlet_sb[:].rearrange("p b t -> p (b t)").unsqueeze(2).to_broadcast([P, H_PASSES * PACK, PAIRS]),
-        )
-        neg_gain = keep.tile([P, H_PASSES, PACK], F32, name="neg_gain")
-        nc.vector.tensor_scalar(out=neg_gain[:], in0=gain_sb[:], scalar1=-1.0, scalar2=None, op0=ALU.mult)
-
-        v_codes = []
-        v_sc = keep.tile([P, S], U8, name="v_sc", align_bytes=64)
-        for a in range(K_PASSES):
-            codes = keep.tile([P, S], U32, name="v_codes%d" % a, align_bytes=64)
-            nc.vector.tensor_copy(out=codes[:], in_=tab[a][:].indirect(offs_sb[:]))
-            v_codes.append(codes)
-            if a == 0:
-                nc.vector.tensor_copy(out=v_sc[:], in_=tab_sc[:].indirect(offs_sb[:]))
-
-        grouped, w_codes, w_sc = {}, {}, {}
-
-        def round_w1(b, a, h, engine, tag):
-            tile = keep.tile([P, 2, P, PACK], BF16, name="w1bf", tag=tag, align_bytes=64)
-            dst = tile[:].rearrange("p t m j -> p m j t")
-            src = raw[b, a][:].rearrange("p j (m t) -> p m j t", t=PACK)[:, :, :, 2 * h : 2 * h + 2]
-            if engine == "vector":
-                nc.vector.tensor_copy(out=dst, in_=src)
-            else:
-                nc.scalar.copy(out=dst, in_=src)
-            grouped[b, a, h] = tile
-
-        def quantize_w1(b, a, h, tag):
-            codes = keep.tile([P, 2 * P], U32, name="w_codes", tag=tag, align_bytes=64)
-            scales = keep.tile([P, 2 * P], U8, name="w_sc%d%d%d" % (b, a, h), align_bytes=64)
-            nc.vector.quantize_mx(
-                out=codes[:].bitcast(FP8X4), scales=scales[:], in_=grouped[b, a, h][:].rearrange("p t m j -> p (t m j)")
-            )
-            w_codes[b, a, h], w_sc[b, a, h] = codes, scales
-
-        banks = {}
-
-        def first_product(b, t, a):
-            for s in range(S // BANK):
-                if a == 0:
-                    banks[b, t, s] = psum.tile([P, BANK], F32, name="bank", tag="bank%d" % (2 * t + s))
-                cols = slice(s * BANK, (s + 1) * BANK)
-                nc.tensor.matmul_mx(
-                    out=banks[b, t, s][:],
-                    lhsT=w_codes[b, a, t // 2][:, (t % 2) * P : (t % 2 + 1) * P].bitcast(FP8X4),
-                    lhsT_scale=w_sc[b, a, t // 2][:, (t % 2) * P : (t % 2 + 1) * P],
-                    rhs=v_codes[a][:, cols].bitcast(FP8X4),
-                    rhs_scale=v_sc[4 * a :, cols],
-                    start=(a == 0),
-                    stop=(a == K_PASSES - 1),
-                )
-
-        act = {}
-
-        def gelu(b, t):
-            tile = keep.tile([P, S], F32, name="act", tag="act", bufs=4)
-            for s in range(S // BANK):
-                nc.scalar.activation(out=tile[:, s * BANK : (s + 1) * BANK], in_=banks[b, t, s][:], func=ACT.Gelu_apprx_tanh)
-            act[b, t] = tile
-
-        diff = [keep.tile([P, PACK, PAIRS], F32, name="diff%d" % b) for b in range(H_PASSES)]
-
-        def pick_pairs(b, t, tag):
-            scaled = keep.tile([P, PAIRS], F32, name="scaled", tag=tag, align_bytes=64)
-            nc.vector.tensor_tensor(
-                out=scaled[:], in0=act[b, t][:].indirect(pos1_sb[:]), in1=inlet_wide[:, PACK * b + t, :], op=ALU.mult
-            )
-            nc.vector.tensor_tensor(
-                out=diff[b][:, t, :], in0=act[b, t][:].indirect(pos2_sb[:]), in1=scaled[:], op=ALU.subtract
-            )
-
-        for a in range(K_PASSES):
-            round_w1(0, a, 0, "vector", "bf0%d0" % a)
-            quantize_w1(0, a, 0, "codes0%d0" % a)
-            round_w1(0, a, 1, "scalar" if a < K_PASSES - 1 else "vector", "bf0%d1" % a)
-            quantize_w1(0, a, 1, "codes0%d1" % a)
-        raw[1, 1] = load_w1(1, 1)
-        raw[1, 2] = load_w1(1, 2)
+        tab[1] = load_table(1)
+        load_w1(0, 0)
+        load_w1(0, 1)
+        tab[2] = load_table(2)
+        for part in (1, 2):
+            for a in range(K_PASSES):
+                load_w1(part, a)
         w4_codes = keep.tile([P, H_PASSES, 2 * N], U8, name="w4_codes", align_bytes=64)
         nc.sync.dma_start(out=w4_codes[:].bitcast(I32), in_=w4_words.rearrange("a p c -> p a c").bitcast(I32))
         for q in range(4):
@@ -164,72 +106,201 @@ def tile_list_raceway_feeder_features_kernel(
                 out=w4_sc[32 * q : 32 * q + 4, :, :].bitcast(I32),
                 in_=w4_scales[:, 4 * q : 4 * q + 4, :].rearrange("a r n -> r a n").bitcast(I32),
             )
+        pos3_sb = load_list(pos3, "pos3_sb")
+        pos4_sb = load_list(pos4, "pos4_sb")
 
-        for a in range(K_PASSES):
-            for t in range(PACK):
-                first_product(0, t, a)
-        gelu(0, 0)
-        pick_pairs(0, 0, "scaled0")
-        gelu(0, 1)
-        pick_pairs(0, 1, "scaled1")
-        round_w1(1, 0, 0, "scalar", "codes020")
-        round_w1(1, 0, 1, "scalar", "codes021")
-        quantize_w1(1, 0, 0, "codes100")
-        quantize_w1(1, 0, 1, "codes101")
-        gelu(0, 2)
-        pick_pairs(0, 2, "codes021")
-        round_w1(1, 1, 0, "scalar", "codes020")
-        round_w1(1, 1, 1, "scalar", "scaled0")
-        quantize_w1(1, 1, 0, "codes110")
-        quantize_w1(1, 1, 1, "codes111")
-        round_w1(1, 2, 0, "vector", "codes020")
-        quantize_w1(1, 2, 0, "codes120")
-        gelu(0, 3)
-        pick_pairs(0, 3, "codes020")
-        round_w1(1, 2, 1, "scalar", "scaled1")
-        quantize_w1(1, 2, 1, "codes121")
-        for t in range(PACK):
-            for a in range(K_PASSES):
-                first_product(1, t, a)
+        inlet_col = by_tile(inlet_raw, 1.0, "inlet_col")
+        neg_gain = by_tile(gain_raw, -1.0, "neg_gain")
+        inlet_wide = keep.tile([P, 8, PAIRS], F32, name="inlet_wide")
+        nc.scalar.copy(out=inlet_wide[:], in_=inlet_col[:].unsqueeze(2).to_broadcast([P, 8, PAIRS]))
 
-        z_bf = [keep.tile([P, PAIRS, PACK], BF16, name="z_bf%d" % b, align_bytes=64) for b in range(H_PASSES)]
-        z0 = keep.tile([P, PACK, PAIRS], F32, name="z0")
-        z_codes, z_sc = {}, {}
+        v_codes = {}
+        v_sc = keep.tile([P, S], U8, name="v_sc", align_bytes=64)
 
-        def apply_gain(t):
-            nc.scalar.activation(out=z0[:, t, :], in_=diff[0][:, t, :], func=ACT.Copy, scale=neg_gain[:, 0, t : t + 1])
+        def gather_table(a, pieces, tag):
+            codes = keep.tile([P, S], U32, name="v_codes", tag=tag, align_bytes=64)
+            width = S // pieces
+            for i in range(pieces):
+                nc.vector.tensor_copy(
+                    out=codes[:, i * width : (i + 1) * width],
+                    in_=tab[a][:].indirect(offs_sb[:, i * width // 16 : (i + 1) * width // 16]),
+                )
+            v_codes[a] = codes
 
-        def quantize_z(b):
-            codes = keep.tile([P, PAIRS], U32, name="z_codes%d" % b, align_bytes=64)
-            scales = keep.tile([P, PAIRS], U8, name="z_sc%d" % b, align_bytes=64)
-            nc.vector.quantize_mx(
-                out=codes[:].bitcast(FP8X4), scales=scales[:], in_=z_bf[b][:].rearrange("p m t -> p (m t)")
+        grouped, w_codes, w_sc = {}, {}, {}
+
+        def bf_tile(tag, n=1):
+            return keep.tile([P, n, 1024], BF16, name="w1bf", tag=tag, align_bytes=64)
+
+        def round_w1(pair, a, engine, dst):
+            if pair < 2:
+                src = raw[pair, a][:].rearrange("p j (m t) -> p m j t", t=PACK)
+                view = dst.rearrange("p (t m j) -> p m j t", t=PACK, j=PACK)
+            else:
+                h = pair - 2
+                src = raw[2, a][:].rearrange("p j (m t) -> p m j t", t=PACK)[:, :, :, 2 * h : 2 * h + 2]
+                view = dst.rearrange("p (t m j) -> p m j t", t=2, j=PACK)
+            if engine == "vector":
+                nc.vector.tensor_copy(out=view, in_=src)
+            else:
+                nc.scalar.copy(out=view, in_=src)
+            grouped[pair, a] = dst
+
+        def quantize_w1(pair, a):
+            codes = keep.tile([P, 2 * P], U32, name="w_codes", tag="codes%d%d" % (pair, a), align_bytes=64)
+            scales = keep.tile([P, 2 * P], U8, name="w_sc", tag="sc%d%d" % (pair, a), align_bytes=64)
+            nc.vector.quantize_mx(out=codes[:].bitcast(FP8X4), scales=scales[:], in_=grouped[pair, a])
+            w_codes[pair, a], w_sc[pair, a] = codes, scales
+
+        banks = {}
+
+        def first_product(i, a, s):
+            if a == 0:
+                banks[i, s] = psum.tile([P, BANK], F32, name="bank", tag="bank%d" % (2 * (i % 4) + s))
+            cols = slice(s * BANK, (s + 1) * BANK)
+            w_cols = slice((i % 2) * P, (i % 2 + 1) * P)
+            nc.tensor.matmul_mx(
+                out=banks[i, s][:],
+                lhsT=w_codes[i // 2, a][:, w_cols].bitcast(FP8X4),
+                lhsT_scale=w_sc[i // 2, a][:, w_cols],
+                rhs=v_codes[a][:, cols].bitcast(FP8X4),
+                rhs_scale=v_sc[4 * a :, cols],
+                start=(a == 0),
+                stop=(a == K_PASSES - 1),
             )
-            z_codes[b], z_sc[b] = codes, scales
 
-        gelu(1, 0)
-        pick_pairs(1, 0, "scaled0")
-        for t in range(PACK - 1):
-            apply_gain(t)
-        gelu(1, 1)
-        pick_pairs(1, 1, "scaled1")
-        apply_gain(PACK - 1)
-        gelu(1, 2)
-        pick_pairs(1, 2, "scaled0")
+        def pair_products(pair, a):
+            for i in (2 * pair, 2 * pair + 1):
+                for s in range(2):
+                    first_product(i, a, s)
+
+        act, diff = {}, {}
+
+        def gelu(i, halves=(0, 1)):
+            if i not in act:
+                act[i] = keep.tile([P, S], F32, name="act", tag="act", bufs=4)
+            for s in halves:
+                nc.scalar.activation(out=act[i][:, s * BANK : (s + 1) * BANK], in_=banks[i, s][:], func=ACT.Gelu_apprx_tanh)
+
+        HALF = PAIRS // 2
+
+        def pick_pairs(i, tag):
+            scaled = keep.tile([P, PAIRS], F32, name="scaled", tag=tag, align_bytes=64)
+            diff[i] = keep.tile([P, PAIRS], F32, name="diff", tag="diff", bufs=4)
+            for e in range(2):
+                cols = slice(e * HALF, (e + 1) * HALF)
+                nc.vector.tensor_tensor(
+                    out=scaled[:, cols],
+                    in0=act[i][:].indirect(pos1_sb[:, 16 * e : 16 * (e + 1)]),
+                    in1=inlet_wide[:, i, cols],
+                    op=ALU.mult,
+                )
+            for e in range(2):
+                cols = slice(e * HALF, (e + 1) * HALF)
+                nc.vector.tensor_tensor(
+                    out=diff[i][:, cols],
+                    in0=act[i][:].indirect(pos2_sb[:, 16 * e : 16 * (e + 1)]),
+                    in1=scaled[:, cols],
+                    op=ALU.subtract,
+                )
+
+        def apply_gain(i, dst, cols=slice(0, PAIRS)):
+            nc.scalar.activation(out=dst[:, cols], in_=diff[i][:, cols], func=ACT.Copy, scale=neg_gain[:, i : i + 1])
+
+        gather_table(0, 1, "v0")
+        nc.vector.tensor_copy(out=v_sc[:], in_=tab_sc[:].indirect(offs_sb[:]))
+        round_w1(0, 2, "scalar", bf_tile("bf02")[:, 0])
+        quantize_w1(0, 2)
+        gather_table(1, 1, "v1")
+        for a in range(2):
+            round_w1(0, a, "scalar", bf_tile("bf0%d" % a)[:, 0])
+            quantize_w1(0, a)
+            pair_products(0, a)
+        gather_table(2, 2, "bf01")
+        for s in range(2):
+            for i in range(2):
+                first_product(i, 2, s)
+                gelu(i, (s,))
+        both = bf_tile("tab2", 2)
+        for a in range(2):
+            round_w1(1, a, "vector", both[:, a])
+        for a in range(2):
+            quantize_w1(1, a)
+            pair_products(1, a)
+        pick_pairs(0, "ringA")
+        round_w1(1, 2, "scalar", bf_tile("codes02")[:, 0])
+        quantize_w1(1, 2)
+        pair_products(1, 2)
+        pick_pairs(1, "codes02")
+        round_w1(2, 0, "scalar", bf_tile("sc02")[:, 0])
+        round_w1(3, 0, "scalar", bf_tile("ringA")[:, 0])
+        quantize_w1(2, 0)
+        quantize_w1(3, 0)
+        gelu(2)
+        pick_pairs(2, "ringA")
+        round_w1(2, 1, "scalar", bf_tile("sc02")[:, 0])
+        round_w1(3, 1, "scalar", bf_tile("codes02")[:, 0])
+        quantize_w1(2, 1)
+        round_w1(2, 2, "vector", bf_tile("sc02")[:, 0])
+        quantize_w1(3, 1)
+        quantize_w1(2, 2)
+        gelu(3)
+        pick_pairs(3, "sc02")
+
+        z_rows = keep.tile([P, PACK, PAIRS], BF16, name="z_rows", tag="z_rows")
+
+        def gain_and_move(u, tag):
+            staged = keep.tile([P, 2, PAIRS], BF16, name="staged", tag=tag, align_bytes=64)
+            for h in range(2):
+                apply_gain(2 * u + h, staged[:, h])
+                for e in range(2):
+                    nc.sync.dma_start(out=z_rows[64 * u : 64 * (u + 1), 2 * h + e, :], in_=staged[64 * e : 64 * (e + 1), h, :])
+
+        gain_and_move(0, "codes12")
+        round_w1(3, 2, "scalar", bf_tile("ringA")[:, 0])
+        quantize_w1(3, 2)
+        for i in range(4, 8):
+            for a in range(K_PASSES):
+                for s in range(2):
+                    first_product(i, a, s)
+
+        z_codes = [keep.tile([P, PAIRS], U32, name="z_codes%d" % b, align_bytes=64) for b in range(H_PASSES)]
+        z_sc = [keep.tile([P, PAIRS], U8, name="z_sc%d" % b, align_bytes=64) for b in range(H_PASSES)]
+
+        def quantize_z(b, z_bf, cols):
+            nc.vector.quantize_mx(
+                out=z_codes[b][:, cols].bitcast(FP8X4), scales=z_sc[b][:, cols], in_=z_bf[:, cols, :].rearrange("p m t -> p (m t)")
+            )
+
+        gelu(4)
+        pick_pairs(4, "ringA")
+        gain_and_move(1, "codes22")
+        gelu(5)
+        pick_pairs(5, "sc02")
+        gelu(6)
+        pick_pairs(6, "ringA")
+        z_bf0 = keep.tile([P, PAIRS, PACK], BF16, name="z_bf0", tag="z_bf0", align_bytes=64)
         nc.scalar.copy(
-            out=z_bf[0][:].rearrange("p (c i) t -> p c t i", i=4),
-            in_=z0[:].rearrange("p t (c i) -> p c t i", i=4),
+            out=z_bf0[:].rearrange("p (c i) t -> p c t i", i=4),
+            in_=z_rows[:].rearrange("p t (c i) -> p c t i", i=4),
         )
-        quantize_z(0)
-        gelu(1, 3)
-        pick_pairs(1, 3, "scaled1")
-        nc.vector.tensor_tensor(
-            out=z_bf[1][:].rearrange("p (c i) t -> p c t i", i=4),
-            in0=diff[1][:].rearrange("p t (c i) -> p c t i", i=4),
-            in1=neg_gain[:, 1, :].unsqueeze(1).unsqueeze(3).to_broadcast([P, PAIRS // 4, PACK, 4]),
-            op=ALU.mult,
-        )
-        quantize_z(1)
+        quantize_z(0, z_bf0, slice(0, PAIRS))
+        gelu(7)
+        pick_pairs(7, "z_bf0")
+        z_rows1 = keep.tile([P, PACK, PAIRS], BF16, name="z_rows", tag="z_rows")
+        for t in range(PACK - 1):
+            apply_gain(4 + t, z_rows1[:, t])
+        z_bf1 = keep.tile([P, PAIRS, PACK], BF16, name="z_bf1", align_bytes=64)
+        for e in range(2):
+            apply_gain(7, z_rows1[:, 3], slice(e * HALF, (e + 1) * HALF))
+        for e in range(2):
+            cols = slice(e * HALF, (e + 1) * HALF)
+            nc.vector.tensor_copy(
+                out=z_bf1[:, cols, :].rearrange("p (c i) t -> p c t i", i=4),
+                in_=z_rows1[:, :, cols].rearrange("p t (c i) -> p c t i", i=4),
+            )
+        for e in range(2):
+            quantize_z(1, z_bf1, slice(e * HALF, (e + 1) * HALF))
 
         for i in range(N_TILES):
             bank = psum.tile([P, BANK], F32, name="bank", tag="bank%d" % i)
@@ -243,10 +314,16 @@ def tile_list_raceway_feeder_features_kernel(
                     start=(b == 0),
                     stop=(b == H_PASSES - 1),
                 )
-            y = keep.tile([P, PAIRS], F32, name="y", tag="y", bufs=4)
+            y = keep.tile([P, PAIRS], F32, name="y", tag="y", bufs=N_TILES)
             nc.scalar.activation(out=y[:], in_=bank[:], func=ACT.Sin)
             left = keep.tile([P, OUT_COLS], F32, name="left", tag="left", bufs=2)
-            nc.vector.tensor_copy(out=left[:], in_=y[:].indirect(pos3_sb[:]))
             res = keep.tile([P, OUT_COLS], F32, name="res", tag="res", bufs=N_TILES)
-            nc.vector.tensor_tensor(out=res[:], in0=y[:].indirect(pos4_sb[:]), in1=left[:], op=ALU.mult)
+            for e in range(2):
+                cols = slice(e * 128, (e + 1) * 128)
+                nc.vector.tensor_copy(out=left[:, cols], in_=y[:].indirect(pos3_sb[:, 8 * e : 8 * (e + 1)]))
+            for e in range(2):
+                cols = slice(e * 128, (e + 1) * 128)
+                nc.vector.tensor_tensor(
+                    out=res[:, cols], in0=y[:].indirect(pos4_sb[:, 8 * e : 8 * (e + 1)]), in1=left[:, cols], op=ALU.mult
+                )
             nc.sync.dma_start(out=out[i * P : (i + 1) * P, :], in_=res[:])

@@ -44,32 +44,34 @@ def tile_list_raceway_feeder_features_kernel(
         w4_sc = keep.tile([P, H_PASSES, N], U8, name="w4_sc", align_bytes=64)
         nc.vector.memset(w4_sc[:].rearrange("p a n -> p (a n)").bitcast(I32), 0)
 
-        def load_vector(dram, name):
-            tile = keep.tile([P, 4, PACK], F32, name=name)
-            for e in range(2):
-                nc.scalar.dma_start(out=tile[64 * e : 64 * (e + 1)], in_=dram.rearrange("(x m t) -> m x t", x=4, t=PACK))
-            return tile
+        vec_rows = keep.tile([P, 3, P], F32, name="vec_rows")
 
-        def by_tile(raw_vec, factor, name):
+        def load_vector(v, dram, queue):
+            quarters = dram.rearrange("(b q c) -> q b c", b=H_PASSES, q=4)
+            queue.dma_start(out=vec_rows[v:P:32, 0:2, :], in_=quarters)
+            for e in range(2):
+                queue.dma_start(out=vec_rows[64 * e + v : 64 * (e + 1) : 32, 2, :], in_=quarters[2 - 2 * e : 4 - 2 * e, 0, :])
+
+        def by_tile(v, factor, name):
             tile = keep.tile([P, 8], F32, name=name)
             for e in range(2):
                 rows = slice(64 * e, 64 * (e + 1))
-                nc.vector.tensor_scalar(
-                    out=tile[rows, 0:4].rearrange("p (u h) -> p u h", u=2),
-                    in0=raw_vec[rows, 0:2, e::2],
-                    scalar1=factor,
-                    scalar2=None,
-                    op0=ALU.mult,
-                )
-                nc.vector.tensor_scalar(
-                    out=tile[rows, 4:8], in0=raw_vec[rows, 2 + e, :], scalar1=factor, scalar2=None, op0=ALU.mult
-                )
+                for u in range(2):
+                    nc.vector.tensor_scalar(
+                        out=tile[rows, 2 * u : 2 * u + 2],
+                        in0=vec_cols[rows, 0 if u == e else 2, e::2, v],
+                        scalar1=factor,
+                        scalar2=None,
+                        op0=ALU.mult,
+                    )
+            nc.vector.tensor_scalar(out=tile[:, 4:8], in0=vec_cols[:, 1, :, v], scalar1=factor, scalar2=None, op0=ALU.mult)
             return tile
 
-        def load_table(a):
-            tile = keep.tile([P, T], U32, name="tab", tag="tab%d" % a, align_bytes=64)
-            nc.sync.dma_start(out=tile[:].bitcast(I32), in_=tab_words[a].rearrange("p t i -> p (t i)").bitcast(I32))
-            return tile
+        tab = {a: keep.tile([P, T], U32, name="tab", tag="tab%d" % a, align_bytes=64) for a in range(K_PASSES)}
+
+        def load_table(a, c0, c1):
+            words = tab_words[a].rearrange("p t i -> p (t i)").bitcast(I32)
+            nc.sync.dma_start(out=tab[a][:].bitcast(I32)[:, c0:c1], in_=words[:, c0:c1])
 
         raw = {}
 
@@ -80,25 +82,27 @@ def tile_list_raceway_feeder_features_kernel(
             nc.sync.dma_start(out=tile[:], in_=rows.rearrange("(p j) c -> p j c", j=PACK))
             raw[part, a] = tile
 
-        inlet_raw = load_vector(inlet, "inlet_raw")
-        gain_raw = load_vector(gain, "gain_raw")
+        load_vector(0, inlet, nc.sync)
+        load_vector(1, gain, nc.scalar)
+        load_table(0, 0, T)
         offs_sb = load_list(offs, "offs_sb")
-        pos1_sb = load_list(pos1, "pos1_sb")
-        pos2_sb = load_list(pos2, "pos2_sb")
-        tab = {0: load_table(0)}
         load_w1(0, 2)
         for q in range(4):
-            nc.sync.dma_start(
+            nc.gpsimd.dma_start(
                 out=tab_sc[32 * q : 32 * q + 4 * K_PASSES, :].bitcast(I32),
                 in_=tab_scales[:, 4 * q : 4 * q + 4, :].bitcast(I32),
             )
-        tab[1] = load_table(1)
+        load_table(1, 0, T)
         load_w1(0, 0)
         load_w1(0, 1)
-        tab[2] = load_table(2)
-        for part in (1, 2):
-            for a in range(K_PASSES):
-                load_w1(part, a)
+        load_table(2, 0, T)
+        load_w1(1, 0)
+        load_w1(1, 1)
+        pos1_sb = load_list(pos1, "pos1_sb")
+        pos2_sb = load_list(pos2, "pos2_sb")
+        load_w1(1, 2)
+        for a in range(K_PASSES):
+            load_w1(2, a)
         w4_codes = keep.tile([P, H_PASSES, 2 * N], U8, name="w4_codes", align_bytes=64)
         nc.sync.dma_start(out=w4_codes[:].bitcast(I32), in_=w4_words.rearrange("a p c -> p a c").bitcast(I32))
         for q in range(4):
@@ -109,10 +113,19 @@ def tile_list_raceway_feeder_features_kernel(
         pos3_sb = load_list(pos3, "pos3_sb")
         pos4_sb = load_list(pos4, "pos4_sb")
 
-        inlet_col = by_tile(inlet_raw, 1.0, "inlet_col")
-        neg_gain = by_tile(gain_raw, -1.0, "neg_gain")
+        vec_sorted = keep.tile([P, 4, PACK, 32], F32, name="vec_sorted", align_bytes=64)
+        nc.vector.memset(vec_sorted[:], 0.0)
+        for q in range(4):
+            rows = slice(32 * q, 32 * q + 2)
+            nc.vector.tensor_copy(out=vec_sorted[rows, 0:3], in_=vec_rows[rows].rearrange("p s (c t) -> p s t c", t=PACK))
+        vec_cols = keep.tile([P, 4, PACK, 32], F32, name="vec_cols", align_bytes=64)
+        nc.vector.transpose(
+            out=vec_cols[:].rearrange("p s t r -> p (s t r)"), in_=vec_sorted[:].rearrange("p s t c -> p (s t c)")
+        )
+        inlet_col = by_tile(0, 1.0, "inlet_col")
+        neg_gain = by_tile(1, -1.0, "neg_gain")
         inlet_wide = keep.tile([P, 8, PAIRS], F32, name="inlet_wide")
-        nc.scalar.copy(out=inlet_wide[:], in_=inlet_col[:].unsqueeze(2).to_broadcast([P, 8, PAIRS]))
+        nc.vector.tensor_copy(out=inlet_wide[:], in_=inlet_col[:].unsqueeze(2).to_broadcast([P, 8, PAIRS]))
 
         v_codes = {}
         v_sc = keep.tile([P, S], U8, name="v_sc", align_bytes=64)
@@ -287,17 +300,19 @@ def tile_list_raceway_feeder_features_kernel(
         quantize_z(0, z_bf0, slice(0, PAIRS))
         gelu(7)
         pick_pairs(7, "z_bf0")
-        z_rows1 = keep.tile([P, PACK, PAIRS], BF16, name="z_rows", tag="z_rows")
+        z_pairs = keep.tile([P, 2, PAIRS, 2], BF16, name="z_pairs", tag="z_rows")
         for t in range(PACK - 1):
-            apply_gain(4 + t, z_rows1[:, t])
+            apply_gain(4 + t, z_pairs[:, t // 2, :, t % 2])
         z_bf1 = keep.tile([P, PAIRS, PACK], BF16, name="z_bf1", align_bytes=64)
         for e in range(2):
-            apply_gain(7, z_rows1[:, 3], slice(e * HALF, (e + 1) * HALF))
+            apply_gain(7, z_pairs[:, 1, :, 1], slice(e * HALF, (e + 1) * HALF))
+        words_in = z_pairs[:].rearrange("p h m e -> p h (m e)").bitcast(I32)
+        words_out = z_bf1[:].bitcast(I32)
         for e in range(2):
             cols = slice(e * HALF, (e + 1) * HALF)
             nc.vector.tensor_copy(
-                out=z_bf1[:, cols, :].rearrange("p (c i) t -> p c t i", i=4),
-                in_=z_rows1[:, :, cols].rearrange("p t (c i) -> p c t i", i=4),
+                out=words_out[:, cols, :].rearrange("p (c i) h -> p c h i", i=4),
+                in_=words_in[:, :, cols].rearrange("p h (c i) -> p c h i", i=4),
             )
         for e in range(2):
             quantize_z(1, z_bf1, slice(e * HALF, (e + 1) * HALF))
@@ -317,7 +332,7 @@ def tile_list_raceway_feeder_features_kernel(
             y = keep.tile([P, PAIRS], F32, name="y", tag="y", bufs=N_TILES)
             nc.scalar.activation(out=y[:], in_=bank[:], func=ACT.Sin)
             left = keep.tile([P, OUT_COLS], F32, name="left", tag="left", bufs=2)
-            res = keep.tile([P, OUT_COLS], F32, name="res", tag="res", bufs=N_TILES)
+            res = keep.tile([P, OUT_COLS], F32, name="res", tag="res", bufs=4)
             for e in range(2):
                 cols = slice(e * 128, (e + 1) * 128)
                 nc.vector.tensor_copy(out=left[:, cols], in_=y[:].indirect(pos3_sb[:, 8 * e : 8 * (e + 1)]))

@@ -22,8 +22,19 @@ K_PASS = P * PACK
 K_PASSES = K // K_PASS
 H_PASSES = H // K_PASS
 BANK = 512
+S_BANKS = S // BANK
+QUADS = 4
+QUAD = P // QUADS
+HALF_P = P // 2
+TILES = H // P
 N_TILES = N // P
+LIST_ROWS = 16
+RUN = 4
+PAIR_WIDTH = 2 * P * PACK
 PARTS = ((0, 256), (256, 512), (512, 1024))
+ACT_BUFS = 4
+HALF = PAIRS // 2
+OUT_HALF = OUT_COLS // 2
 
 
 def tile_list_raceway_feeder_features_kernel(
@@ -33,6 +44,7 @@ def tile_list_raceway_feeder_features_kernel(
     with ExitStack() as ctx:
         keep = ctx.enter_context(tc.tile_pool(name="keep", bufs=1))
         psum = ctx.enter_context(tc.psum_pool(name="psum", bufs=1))
+
 
         def load_list(dram, name):
             tile = keep.tile(list(dram.shape), U16, name=name)
@@ -47,55 +59,42 @@ def tile_list_raceway_feeder_features_kernel(
         vec_rows = keep.tile([P, 3, P], F32, name="vec_rows")
 
         def load_vector(v, dram, queue):
-            quarters = dram.rearrange("(b q c) -> q b c", b=H_PASSES, q=4)
-            queue.dma_start(out=vec_rows[v:P:32, 0:2, :], in_=quarters)
+            quarters = dram.rearrange("(b q c) -> q b c", b=H_PASSES, q=QUADS)
+            queue.dma_start(out=vec_rows[v:P:QUAD, 0:2, :], in_=quarters)
             for e in range(2):
-                queue.dma_start(out=vec_rows[64 * e + v : 64 * (e + 1) : 32, 2, :], in_=quarters[2 - 2 * e : 4 - 2 * e, 0, :])
-
-        def by_tile(v, factor, name):
-            tile = keep.tile([P, 8], F32, name=name)
-            for e in range(2):
-                rows = slice(64 * e, 64 * (e + 1))
-                for u in range(2):
-                    nc.vector.tensor_scalar(
-                        out=tile[rows, 2 * u : 2 * u + 2],
-                        in0=vec_cols[rows, 0 if u == e else 2, e::2, v],
-                        scalar1=factor,
-                        scalar2=None,
-                        op0=ALU.mult,
-                    )
-            nc.vector.tensor_scalar(out=tile[:, 4:8], in0=vec_cols[:, 1, :, v], scalar1=factor, scalar2=None, op0=ALU.mult)
-            return tile
+                queue.dma_start(
+                    out=vec_rows[HALF_P * e + v : HALF_P * (e + 1) : QUAD, 2, :], in_=quarters[2 - 2 * e : 4 - 2 * e, 0, :]
+                )
 
         tab = {a: keep.tile([P, T], U32, name="tab", tag="tab%d" % a, align_bytes=64) for a in range(K_PASSES)}
 
-        def load_table(a, c0, c1):
+        def load_table(a):
             words = tab_words[a].rearrange("p t i -> p (t i)").bitcast(I32)
-            nc.sync.dma_start(out=tab[a][:].bitcast(I32)[:, c0:c1], in_=words[:, c0:c1])
+            nc.sync.dma_start(out=tab[a][:].bitcast(I32), in_=words)
 
         raw = {}
 
         def load_w1(part, a):
             c0, c1 = PARTS[part]
             tile = keep.tile([P, PACK, c1 - c0], F32, name="w1raw%d%d" % (part, a))
-            rows = w1[a * K_PASS : (a + 1) * K_PASS, c0:c1]
-            nc.sync.dma_start(out=tile[:], in_=rows.rearrange("(p j) c -> p j c", j=PACK))
+            block = w1[a * K_PASS : (a + 1) * K_PASS, c0:c1]
+            nc.sync.dma_start(out=tile[:], in_=block.rearrange("(p j) c -> p j c", j=PACK))
             raw[part, a] = tile
 
         load_vector(0, inlet, nc.sync)
         load_vector(1, gain, nc.scalar)
-        load_table(0, 0, T)
+        load_table(0)
         offs_sb = load_list(offs, "offs_sb")
         load_w1(0, 2)
-        for q in range(4):
+        for q in range(QUADS):
             nc.gpsimd.dma_start(
-                out=tab_sc[32 * q : 32 * q + 4 * K_PASSES, :].bitcast(I32),
+                out=tab_sc[QUAD * q : QUAD * q + 4 * K_PASSES, :].bitcast(I32),
                 in_=tab_scales[:, 4 * q : 4 * q + 4, :].bitcast(I32),
             )
-        load_table(1, 0, T)
+        load_table(1)
         load_w1(0, 0)
         load_w1(0, 1)
-        load_table(2, 0, T)
+        load_table(2)
         load_w1(1, 0)
         load_w1(1, 1)
         pos1_sb = load_list(pos1, "pos1_sb")
@@ -105,27 +104,48 @@ def tile_list_raceway_feeder_features_kernel(
             load_w1(2, a)
         w4_codes = keep.tile([P, H_PASSES, 2 * N], U8, name="w4_codes", align_bytes=64)
         nc.sync.dma_start(out=w4_codes[:].bitcast(I32), in_=w4_words.rearrange("a p c -> p a c").bitcast(I32))
-        for q in range(4):
+        for q in range(QUADS):
             nc.sync.dma_start(
-                out=w4_sc[32 * q : 32 * q + 4, :, :].bitcast(I32),
+                out=w4_sc[QUAD * q : QUAD * q + 4, :, :].bitcast(I32),
                 in_=w4_scales[:, 4 * q : 4 * q + 4, :].rearrange("a r n -> r a n").bitcast(I32),
             )
         pos3_sb = load_list(pos3, "pos3_sb")
         pos4_sb = load_list(pos4, "pos4_sb")
 
-        vec_sorted = keep.tile([P, 4, PACK, 32], F32, name="vec_sorted", align_bytes=64)
+
+        vec_sorted = keep.tile([P, 4, PACK, QUAD], F32, name="vec_sorted", align_bytes=64)
         nc.vector.memset(vec_sorted[:], 0.0)
-        for q in range(4):
-            rows = slice(32 * q, 32 * q + 2)
+        for q in range(QUADS):
+            rows = slice(QUAD * q, QUAD * q + 2)
             nc.vector.tensor_copy(out=vec_sorted[rows, 0:3], in_=vec_rows[rows].rearrange("p s (c t) -> p s t c", t=PACK))
-        vec_cols = keep.tile([P, 4, PACK, 32], F32, name="vec_cols", align_bytes=64)
+        vec_cols = keep.tile([P, 4, PACK, QUAD], F32, name="vec_cols", align_bytes=64)
         nc.vector.transpose(
             out=vec_cols[:].rearrange("p s t r -> p (s t r)"), in_=vec_sorted[:].rearrange("p s t c -> p (s t c)")
         )
+
+        def by_tile(v, sign, name):
+            tile = keep.tile([P, TILES], F32, name=name)
+            for e in range(2):
+                rows = slice(HALF_P * e, HALF_P * (e + 1))
+                for u in range(2):
+                    nc.vector.tensor_scalar(
+                        out=tile[rows, 2 * u : 2 * u + 2],
+                        in0=vec_cols[rows, 0 if u == e else 2, e::2, v],
+                        scalar1=sign,
+                        scalar2=None,
+                        op0=ALU.mult,
+                    )
+            nc.vector.tensor_scalar(out=tile[:, PACK:], in0=vec_cols[:, 1, :, v], scalar1=sign, scalar2=None, op0=ALU.mult)
+            return tile
+
         inlet_col = by_tile(0, 1.0, "inlet_col")
         neg_gain = by_tile(1, -1.0, "neg_gain")
-        inlet_wide = keep.tile([P, 8, PAIRS], F32, name="inlet_wide")
-        nc.vector.tensor_copy(out=inlet_wide[:], in_=inlet_col[:].unsqueeze(2).to_broadcast([P, 8, PAIRS]))
+        inlet_wide = keep.tile([P, TILES, PAIRS], F32, name="inlet_wide")
+        nc.vector.tensor_copy(out=inlet_wide[:], in_=inlet_col[:].unsqueeze(2).to_broadcast([P, TILES, PAIRS]))
+
+
+        def entries(list_sb, first, count):
+            return list_sb[:, first // LIST_ROWS : (first + count) // LIST_ROWS]
 
         v_codes = {}
         v_sc = keep.tile([P, S], U8, name="v_sc", align_bytes=64)
@@ -133,19 +153,18 @@ def tile_list_raceway_feeder_features_kernel(
         def gather_table(a, pieces, tag):
             codes = keep.tile([P, S], U32, name="v_codes", tag=tag, align_bytes=64)
             width = S // pieces
-            for i in range(pieces):
+            for n in range(pieces):
                 nc.vector.tensor_copy(
-                    out=codes[:, i * width : (i + 1) * width],
-                    in_=tab[a][:].indirect(offs_sb[:, i * width // 16 : (i + 1) * width // 16]),
+                    out=codes[:, n * width : (n + 1) * width], in_=tab[a][:].indirect(entries(offs_sb, n * width, width))
                 )
             v_codes[a] = codes
 
-        grouped, w_codes, w_sc = {}, {}, {}
+        rounded, w_codes, w_sc = {}, {}, {}
 
-        def bf_tile(tag, n=1):
-            return keep.tile([P, n, 1024], BF16, name="w1bf", tag=tag, align_bytes=64)
+        def bf_tile(tag, passes=1):
+            return keep.tile([P, passes, PAIR_WIDTH], BF16, name="w1bf", tag=tag, align_bytes=64)
 
-        def round_w1(pair, a, engine, dst):
+        def round_w1(pair, a, copy, dst):
             if pair < 2:
                 src = raw[pair, a][:].rearrange("p j (m t) -> p m j t", t=PACK)
                 view = dst.rearrange("p (t m j) -> p m j t", t=PACK, j=PACK)
@@ -153,23 +172,20 @@ def tile_list_raceway_feeder_features_kernel(
                 h = pair - 2
                 src = raw[2, a][:].rearrange("p j (m t) -> p m j t", t=PACK)[:, :, :, 2 * h : 2 * h + 2]
                 view = dst.rearrange("p (t m j) -> p m j t", t=2, j=PACK)
-            if engine == "vector":
-                nc.vector.tensor_copy(out=view, in_=src)
-            else:
-                nc.scalar.copy(out=view, in_=src)
-            grouped[pair, a] = dst
+            copy(out=view, in_=src)
+            rounded[pair, a] = dst
 
         def quantize_w1(pair, a):
             codes = keep.tile([P, 2 * P], U32, name="w_codes", tag="codes%d%d" % (pair, a), align_bytes=64)
             scales = keep.tile([P, 2 * P], U8, name="w_sc", tag="sc%d%d" % (pair, a), align_bytes=64)
-            nc.vector.quantize_mx(out=codes[:].bitcast(FP8X4), scales=scales[:], in_=grouped[pair, a])
+            nc.vector.quantize_mx(out=codes[:].bitcast(FP8X4), scales=scales[:], in_=rounded[pair, a])
             w_codes[pair, a], w_sc[pair, a] = codes, scales
 
         banks = {}
 
         def first_product(i, a, s):
             if a == 0:
-                banks[i, s] = psum.tile([P, BANK], F32, name="bank", tag="bank%d" % (2 * (i % 4) + s))
+                banks[i, s] = psum.tile([P, BANK], F32, name="bank", tag="bank%d" % (S_BANKS * (i % ACT_BUFS) + s))
             cols = slice(s * BANK, (s + 1) * BANK)
             w_cols = slice((i % 2) * P, (i % 2 + 1) * P)
             nc.tensor.matmul_mx(
@@ -182,80 +198,97 @@ def tile_list_raceway_feeder_features_kernel(
                 stop=(a == K_PASSES - 1),
             )
 
-        def pair_products(pair, a):
+        def pair_pass(pair, a):
             for i in (2 * pair, 2 * pair + 1):
-                for s in range(2):
+                for s in range(S_BANKS):
                     first_product(i, a, s)
 
-        act, diff = {}, {}
+        def pair_by_tile(pair):
+            for i in (2 * pair, 2 * pair + 1):
+                for a in range(K_PASSES):
+                    for s in range(S_BANKS):
+                        first_product(i, a, s)
 
-        def gelu(i, halves=(0, 1)):
-            if i not in act:
-                act[i] = keep.tile([P, S], F32, name="act", tag="act", bufs=4)
-            for s in halves:
-                nc.scalar.activation(out=act[i][:, s * BANK : (s + 1) * BANK], in_=banks[i, s][:], func=ACT.Gelu_apprx_tanh)
+        act, scaled, diff = {}, {}, {}
 
-        HALF = PAIRS // 2
+        def gelu_bank(i, s):
+            if s == 0:
+                act[i] = keep.tile([P, S], F32, name="act", tag="act", bufs=ACT_BUFS)
+            nc.scalar.activation(out=act[i][:, s * BANK : (s + 1) * BANK], in_=banks[i, s][:], func=ACT.Gelu_apprx_tanh)
 
-        def pick_pairs(i, tag):
-            scaled = keep.tile([P, PAIRS], F32, name="scaled", tag=tag, align_bytes=64)
-            diff[i] = keep.tile([P, PAIRS], F32, name="diff", tag="diff", bufs=4)
-            for e in range(2):
-                cols = slice(e * HALF, (e + 1) * HALF)
+        def gelu(i):
+            for s in range(S_BANKS):
+                gelu_bank(i, s)
+
+        def pick_inlet(i, tag):
+            scaled[i] = keep.tile([P, PAIRS], F32, name="scaled", tag=tag, align_bytes=64)
+            for m0 in (0, HALF):
+                cols = slice(m0, m0 + HALF)
                 nc.vector.tensor_tensor(
-                    out=scaled[:, cols],
-                    in0=act[i][:].indirect(pos1_sb[:, 16 * e : 16 * (e + 1)]),
+                    out=scaled[i][:, cols],
+                    in0=act[i][:].indirect(entries(pos1_sb, m0, HALF)),
                     in1=inlet_wide[:, i, cols],
                     op=ALU.mult,
                 )
-            for e in range(2):
-                cols = slice(e * HALF, (e + 1) * HALF)
+
+        def pick_outlet(i, tag):
+            diff[i] = keep.tile([P, PAIRS], F32, name="diff", tag=tag, align_bytes=64)
+            for m0 in (0, HALF):
+                cols = slice(m0, m0 + HALF)
                 nc.vector.tensor_tensor(
                     out=diff[i][:, cols],
-                    in0=act[i][:].indirect(pos2_sb[:, 16 * e : 16 * (e + 1)]),
-                    in1=scaled[:, cols],
+                    in0=act[i][:].indirect(entries(pos2_sb, m0, HALF)),
+                    in1=scaled[i][:, cols],
                     op=ALU.subtract,
                 )
 
-        def apply_gain(i, dst, cols=slice(0, PAIRS)):
+        def pick_pairs(i, tag):
+            pick_inlet(i, tag)
+            pick_outlet(i, "diff%d" % (i % ACT_BUFS))
+
+        def apply_gain(i, dst, cols):
             nc.scalar.activation(out=dst[:, cols], in_=diff[i][:, cols], func=ACT.Copy, scale=neg_gain[:, i : i + 1])
+
+        on_scalar, on_vector = nc.scalar.copy, nc.vector.tensor_copy
+        every_pair = slice(0, PAIRS)
+
 
         gather_table(0, 1, "v0")
         nc.vector.tensor_copy(out=v_sc[:], in_=tab_sc[:].indirect(offs_sb[:]))
-        round_w1(0, 2, "scalar", bf_tile("bf02")[:, 0])
+        round_w1(0, 2, on_scalar, bf_tile("bf02")[:, 0])
         quantize_w1(0, 2)
         gather_table(1, 1, "v1")
         for a in range(2):
-            round_w1(0, a, "scalar", bf_tile("bf0%d" % a)[:, 0])
+            round_w1(0, a, on_scalar, bf_tile("bf0%d" % a)[:, 0])
             quantize_w1(0, a)
-            pair_products(0, a)
-        gather_table(2, 2, "bf01")
-        for s in range(2):
+            pair_pass(0, a)
+        gather_table(2, S_BANKS, "bf01")
+        for s in range(S_BANKS):
             for i in range(2):
                 first_product(i, 2, s)
-                gelu(i, (s,))
+                gelu_bank(i, s)
+
+
         both = bf_tile("tab2", 2)
         for a in range(2):
-            round_w1(1, a, "vector", both[:, a])
+            round_w1(1, a, on_vector, both[:, a])
         for a in range(2):
             quantize_w1(1, a)
-            pair_products(1, a)
-        pick_pairs(0, "ringA")
-        round_w1(1, 2, "scalar", bf_tile("codes02")[:, 0])
+            pair_pass(1, a)
+        pick_pairs(0, "ring")
+        round_w1(1, 2, on_scalar, bf_tile("codes02")[:, 0])
         quantize_w1(1, 2)
-        pair_products(1, 2)
+        pair_pass(1, 2)
         pick_pairs(1, "codes02")
-        round_w1(2, 0, "scalar", bf_tile("sc02")[:, 0])
-        round_w1(3, 0, "scalar", bf_tile("ringA")[:, 0])
+        round_w1(2, 0, on_scalar, bf_tile("sc02")[:, 0])
         quantize_w1(2, 0)
-        quantize_w1(3, 0)
         gelu(2)
-        pick_pairs(2, "ringA")
-        round_w1(2, 1, "scalar", bf_tile("sc02")[:, 0])
-        round_w1(3, 1, "scalar", bf_tile("codes02")[:, 0])
+        pick_pairs(2, "sc02")
+        round_w1(2, 1, on_scalar, bf_tile("codes02")[:, 0])
+        round_w1(3, 0, on_scalar, bf_tile("ring")[:, 0])
         quantize_w1(2, 1)
-        round_w1(2, 2, "vector", bf_tile("sc02")[:, 0])
-        quantize_w1(3, 1)
+        round_w1(2, 2, on_vector, bf_tile("sc02")[:, 0])
+        quantize_w1(3, 0)
         quantize_w1(2, 2)
         gelu(3)
         pick_pairs(3, "sc02")
@@ -265,57 +298,67 @@ def tile_list_raceway_feeder_features_kernel(
         def gain_and_move(u, tag):
             staged = keep.tile([P, 2, PAIRS], BF16, name="staged", tag=tag, align_bytes=64)
             for h in range(2):
-                apply_gain(2 * u + h, staged[:, h])
+                apply_gain(2 * u + h, staged[:, h], every_pair)
                 for e in range(2):
-                    nc.sync.dma_start(out=z_rows[64 * u : 64 * (u + 1), 2 * h + e, :], in_=staged[64 * e : 64 * (e + 1), h, :])
+                    nc.sync.dma_start(
+                        out=z_rows[HALF_P * u : HALF_P * (u + 1), 2 * h + e, :],
+                        in_=staged[HALF_P * e : HALF_P * (e + 1), h, :],
+                    )
 
         gain_and_move(0, "codes12")
-        round_w1(3, 2, "scalar", bf_tile("ringA")[:, 0])
-        quantize_w1(3, 2)
-        for i in range(4, 8):
-            for a in range(K_PASSES):
-                for s in range(2):
-                    first_product(i, a, s)
+        round_w1(3, 1, on_scalar, bf_tile("codes02")[:, 0])
+        quantize_w1(3, 1)
+
+
+        pair_by_tile(2)
 
         z_codes = [keep.tile([P, PAIRS], U32, name="z_codes%d" % b, align_bytes=64) for b in range(H_PASSES)]
         z_sc = [keep.tile([P, PAIRS], U8, name="z_sc%d" % b, align_bytes=64) for b in range(H_PASSES)]
 
         def quantize_z(b, z_bf, cols):
             nc.vector.quantize_mx(
-                out=z_codes[b][:, cols].bitcast(FP8X4), scales=z_sc[b][:, cols], in_=z_bf[:, cols, :].rearrange("p m t -> p (m t)")
+                out=z_codes[b][:, cols].bitcast(FP8X4),
+                scales=z_sc[b][:, cols],
+                in_=z_bf[:, cols, :].rearrange("p m t -> p (m t)"),
             )
 
         gelu(4)
-        pick_pairs(4, "ringA")
-        gain_and_move(1, "codes22")
+        pick_pairs(4, "codes02")
+        round_w1(3, 2, on_scalar, bf_tile("sc22")[:, 0])
+        quantize_w1(3, 2)
+        pair_by_tile(3)
         gelu(5)
-        pick_pairs(5, "sc02")
+        pick_pairs(5, "sc22")
+        gain_and_move(1, "codes22")
         gelu(6)
-        pick_pairs(6, "ringA")
-        z_bf0 = keep.tile([P, PAIRS, PACK], BF16, name="z_bf0", tag="z_bf0", align_bytes=64)
-        nc.scalar.copy(
-            out=z_bf0[:].rearrange("p (c i) t -> p c t i", i=4),
-            in_=z_rows[:].rearrange("p t (c i) -> p c t i", i=4),
-        )
-        quantize_z(0, z_bf0, slice(0, PAIRS))
+        pick_pairs(6, "ring")
         gelu(7)
-        pick_pairs(7, "z_bf0")
+        pick_inlet(7, "sc02")
+        z_bf0 = keep.tile([P, PAIRS, PACK], BF16, name="z_bf0", tag="codes32", align_bytes=64)
+        nc.scalar.copy(
+            out=z_bf0[:].rearrange("p (c i) t -> p c t i", i=RUN),
+            in_=z_rows[:].rearrange("p t (c i) -> p c t i", i=RUN),
+        )
+        quantize_z(0, z_bf0, every_pair)
+        pick_outlet(7, "codes32")
+
         z_pairs = keep.tile([P, 2, PAIRS, 2], BF16, name="z_pairs", tag="z_rows")
         for t in range(PACK - 1):
-            apply_gain(4 + t, z_pairs[:, t // 2, :, t % 2])
+            apply_gain(PACK + t, z_pairs[:, t // 2, :, t % 2], every_pair)
         z_bf1 = keep.tile([P, PAIRS, PACK], BF16, name="z_bf1", align_bytes=64)
-        for e in range(2):
-            apply_gain(7, z_pairs[:, 1, :, 1], slice(e * HALF, (e + 1) * HALF))
+        halves = [slice(m0, m0 + HALF) for m0 in (0, HALF)]
+        for cols in halves:
+            apply_gain(TILES - 1, z_pairs[:, 1, :, 1], cols)
         words_in = z_pairs[:].rearrange("p h m e -> p h (m e)").bitcast(I32)
         words_out = z_bf1[:].bitcast(I32)
-        for e in range(2):
-            cols = slice(e * HALF, (e + 1) * HALF)
+        for cols in halves:
             nc.vector.tensor_copy(
-                out=words_out[:, cols, :].rearrange("p (c i) h -> p c h i", i=4),
-                in_=words_in[:, :, cols].rearrange("p h (c i) -> p c h i", i=4),
+                out=words_out[:, cols, :].rearrange("p (c i) h -> p c h i", i=RUN),
+                in_=words_in[:, :, cols].rearrange("p h (c i) -> p c h i", i=RUN),
             )
-        for e in range(2):
-            quantize_z(1, z_bf1, slice(e * HALF, (e + 1) * HALF))
+        for cols in halves:
+            quantize_z(1, z_bf1, cols)
+
 
         for i in range(N_TILES):
             bank = psum.tile([P, BANK], F32, name="bank", tag="bank%d" % i)
@@ -332,13 +375,13 @@ def tile_list_raceway_feeder_features_kernel(
             y = keep.tile([P, PAIRS], F32, name="y", tag="y", bufs=N_TILES)
             nc.scalar.activation(out=y[:], in_=bank[:], func=ACT.Sin)
             left = keep.tile([P, OUT_COLS], F32, name="left", tag="left", bufs=2)
-            res = keep.tile([P, OUT_COLS], F32, name="res", tag="res", bufs=4)
-            for e in range(2):
-                cols = slice(e * 128, (e + 1) * 128)
-                nc.vector.tensor_copy(out=left[:, cols], in_=y[:].indirect(pos3_sb[:, 8 * e : 8 * (e + 1)]))
-            for e in range(2):
-                cols = slice(e * 128, (e + 1) * 128)
+            res = keep.tile([P, OUT_COLS], F32, name="res", tag="res", bufs=N_TILES)
+            for j0 in (0, OUT_HALF):
+                cols = slice(j0, j0 + OUT_HALF)
+                nc.vector.tensor_copy(out=left[:, cols], in_=y[:].indirect(entries(pos3_sb, j0, OUT_HALF)))
+            for j0 in (0, OUT_HALF):
+                cols = slice(j0, j0 + OUT_HALF)
                 nc.vector.tensor_tensor(
-                    out=res[:, cols], in0=y[:].indirect(pos4_sb[:, 8 * e : 8 * (e + 1)]), in1=left[:, cols], op=ALU.mult
+                    out=res[:, cols], in0=y[:].indirect(entries(pos4_sb, j0, OUT_HALF)), in1=left[:, cols], op=ALU.mult
                 )
             nc.sync.dma_start(out=out[i * P : (i + 1) * P, :], in_=res[:])

from contextlib import ExitStack

import concourse.mybir as mybir

K, T, S, H, PAIRS, N, OUT_COLS = 1536, 4096, 1024, 1024, 512, 768, 256
FLOPS = 2 * K * H * S + 2 * H * N * PAIRS

F32 = mybir.dt.float32
BF16 = mybir.dt.bfloat16
I32 = mybir.dt.int32
U32 = mybir.dt.uint32
U16 = mybir.dt.uint16
U8 = mybir.dt.uint8
FP8X4 = mybir.dt.float8_e4m3fn_x4
FP4X4 = mybir.dt.float4_e2m1fn_x4
ACT = mybir.ActivationFunctionType
ALU = mybir.AluOpType

P = 128
PACK = 4
K_PASS = P * PACK
K_PASSES = K // K_PASS
H_PASSES = H // K_PASS
BANK = 512
S_BANKS = S // BANK
QUADS = 4
QUAD = P // QUADS
HALF_P = P // 2
TILES = H // P
N_TILES = N // P
LIST_ROWS = 16
RUN = 4
PAIR_WIDTH = 2 * P * PACK
PARTS = ((0, 256), (256, 512), (512, 1024))
ACT_BUFS = 4
HALF = PAIRS // 2
OUT_HALF = OUT_COLS // 2


def tile_list_raceway_feeder_features_kernel(
    tc, tab_words, tab_scales, w1, gain, inlet, w4_words, w4_scales, offs, pos1, pos2, pos3, pos4, out
):
    nc = tc.nc
    with ExitStack() as ctx:
        keep = ctx.enter_context(tc.tile_pool(name="keep", bufs=1))
        psum = ctx.enter_context(tc.psum_pool(name="psum", bufs=1))


        def load_list(dram, name):
            tile = keep.tile(list(dram.shape), U16, name=name)
            nc.sync.dma_start(tile[:], dram)
            return tile

        tab_sc = keep.tile([P, T], U8, name="tab_sc", align_bytes=64)
        nc.vector.memset(tab_sc[:].bitcast(I32), 0)
        w4_sc = keep.tile([P, H_PASSES, N], U8, name="w4_sc", align_bytes=64)
        nc.vector.memset(w4_sc[:].rearrange("p a n -> p (a n)").bitcast(I32), 0)

        vec_rows = keep.tile([P, 3, P], F32, name="vec_rows")

        def load_vector(v, dram, queue):
            quarters = dram.rearrange("(b q c) -> q b c", b=H_PASSES, q=QUADS)
            queue.dma_start(out=vec_rows[v:P:QUAD, 0:2, :], in_=quarters)
            for e in range(2):
                queue.dma_start(
                    out=vec_rows[HALF_P * e + v : HALF_P * (e + 1) : QUAD, 2, :], in_=quarters[2 - 2 * e : 4 - 2 * e, 0, :]
                )

        tab = {a: keep.tile([P, T], U32, name="tab", tag="tab%d" % a, align_bytes=64) for a in range(K_PASSES)}

        def load_table(a):
            words = tab_words[a].rearrange("p t i -> p (t i)").bitcast(I32)
            nc.sync.dma_start(out=tab[a][:].bitcast(I32), in_=words)

        raw = {}

        def load_w1(part, a):
            c0, c1 = PARTS[part]
            tile = keep.tile([P, PACK, c1 - c0], F32, name="w1raw%d%d" % (part, a))
            block = w1[a * K_PASS : (a + 1) * K_PASS, c0:c1]
            nc.sync.dma_start(out=tile[:], in_=block.rearrange("(p j) c -> p j c", j=PACK))
            raw[part, a] = tile

        load_vector(0, inlet, nc.sync)
        load_vector(1, gain, nc.scalar)
        load_table(0)
        offs_sb = load_list(offs, "offs_sb")
        load_w1(0, 2)
        for q in range(QUADS):
            nc.gpsimd.dma_start(
                out=tab_sc[QUAD * q : QUAD * q + 4 * K_PASSES, :].bitcast(I32),
                in_=tab_scales[:, 4 * q : 4 * q + 4, :].bitcast(I32),
            )
        load_table(1)
        load_w1(0, 0)
        load_w1(0, 1)
        load_table(2)
        load_w1(1, 0)
        load_w1(1, 1)
        pos1_sb = load_list(pos1, "pos1_sb")
        pos2_sb = load_list(pos2, "pos2_sb")
        load_w1(1, 2)
        for a in range(K_PASSES):
            load_w1(2, a)
        w4_codes = keep.tile([P, H_PASSES, 2 * N], U8, name="w4_codes", align_bytes=64)
        nc.sync.dma_start(out=w4_codes[:].bitcast(I32), in_=w4_words.rearrange("a p c -> p a c").bitcast(I32))
        for q in range(QUADS):
            nc.sync.dma_start(
                out=w4_sc[QUAD * q : QUAD * q + 4, :, :].bitcast(I32),
                in_=w4_scales[:, 4 * q : 4 * q + 4, :].rearrange("a r n -> r a n").bitcast(I32),
            )
        pos3_sb = load_list(pos3, "pos3_sb")
        pos4_sb = load_list(pos4, "pos4_sb")


        vec_sorted = keep.tile([P, 4, PACK, QUAD], F32, name="vec_sorted", align_bytes=64)
        nc.vector.memset(vec_sorted[:], 0.0)
        for q in range(QUADS):
            rows = slice(QUAD * q, QUAD * q + 2)
            nc.vector.tensor_copy(out=vec_sorted[rows, 0:3], in_=vec_rows[rows].rearrange("p s (c t) -> p s t c", t=PACK))
        vec_cols = keep.tile([P, 4, PACK, QUAD], F32, name="vec_cols", align_bytes=64)
        nc.vector.transpose(
            out=vec_cols[:].rearrange("p s t r -> p (s t r)"), in_=vec_sorted[:].rearrange("p s t c -> p (s t c)")
        )

        def by_tile(v, sign, name):
            tile = keep.tile([P, TILES], F32, name=name)
            for e in range(2):
                rows = slice(HALF_P * e, HALF_P * (e + 1))
                for u in range(2):
                    nc.vector.tensor_scalar(
                        out=tile[rows, 2 * u : 2 * u + 2],
                        in0=vec_cols[rows, 0 if u == e else 2, e::2, v],
                        scalar1=sign,
                        scalar2=None,
                        op0=ALU.mult,
                    )
            nc.vector.tensor_scalar(out=tile[:, PACK:], in0=vec_cols[:, 1, :, v], scalar1=sign, scalar2=None, op0=ALU.mult)
            return tile

        inlet_col = by_tile(0, 1.0, "inlet_col")
        neg_gain = by_tile(1, -1.0, "neg_gain")
        inlet_wide = keep.tile([P, TILES, PAIRS], F32, name="inlet_wide")
        nc.vector.tensor_copy(out=inlet_wide[:], in_=inlet_col[:].unsqueeze(2).to_broadcast([P, TILES, PAIRS]))


        def entries(list_sb, first, count):
            return list_sb[:, first // LIST_ROWS : (first + count) // LIST_ROWS]

        v_codes = {}
        v_sc = keep.tile([P, S], U8, name="v_sc", align_bytes=64)

        def gather_table(a, pieces, tag):
            codes = keep.tile([P, S], U32, name="v_codes", tag=tag, align_bytes=64)
            width = S // pieces
            for n in range(pieces):
                nc.vector.tensor_copy(
                    out=codes[:, n * width : (n + 1) * width], in_=tab[a][:].indirect(entries(offs_sb, n * width, width))
                )
            v_codes[a] = codes

        rounded, w_codes, w_sc = {}, {}, {}

        def bf_tile(tag, passes=1):
            return keep.tile([P, passes, PAIR_WIDTH], BF16, name="w1bf", tag=tag, align_bytes=64)

        def round_w1(pair, a, copy, dst):
            if pair < 2:
                src = raw[pair, a][:].rearrange("p j (m t) -> p m j t", t=PACK)
                view = dst.rearrange("p (t m j) -> p m j t", t=PACK, j=PACK)
            else:
                h = pair - 2
                src = raw[2, a][:].rearrange("p j (m t) -> p m j t", t=PACK)[:, :, :, 2 * h : 2 * h + 2]
                view = dst.rearrange("p (t m j) -> p m j t", t=2, j=PACK)
            copy(out=view, in_=src)
            rounded[pair, a] = dst

        def quantize_w1(pair, a):
            codes = keep.tile([P, 2 * P], U32, name="w_codes", tag="codes%d%d" % (pair, a), align_bytes=64)
            scales = keep.tile([P, 2 * P], U8, name="w_sc", tag="sc%d%d" % (pair, a), align_bytes=64)
            nc.vector.quantize_mx(out=codes[:].bitcast(FP8X4), scales=scales[:], in_=rounded[pair, a])
            w_codes[pair, a], w_sc[pair, a] = codes, scales

        banks = {}

        def first_product(i, a, s):
            if a == 0:
                banks[i, s] = psum.tile([P, BANK], F32, name="bank", tag="bank%d" % (S_BANKS * (i % ACT_BUFS) + s))
            cols = slice(s * BANK, (s + 1) * BANK)
            w_cols = slice((i % 2) * P, (i % 2 + 1) * P)
            nc.tensor.matmul_mx(
                out=banks[i, s][:],
                lhsT=w_codes[i // 2, a][:, w_cols].bitcast(FP8X4),
                lhsT_scale=w_sc[i // 2, a][:, w_cols],
                rhs=v_codes[a][:, cols].bitcast(FP8X4),
                rhs_scale=v_sc[4 * a :, cols],
                start=(a == 0),
                stop=(a == K_PASSES - 1),
            )

        def pair_pass(pair, a):
            for i in (2 * pair, 2 * pair + 1):
                for s in range(S_BANKS):
                    first_product(i, a, s)

        def pair_by_tile(pair):
            for i in (2 * pair, 2 * pair + 1):
                for a in range(K_PASSES):
                    for s in range(S_BANKS):
                        first_product(i, a, s)

        act, scaled, diff = {}, {}, {}

        def gelu_bank(i, s):
            if s == 0:
                act[i] = keep.tile([P, S], F32, name="act", tag="act", bufs=ACT_BUFS)
            nc.scalar.activation(out=act[i][:, s * BANK : (s + 1) * BANK], in_=banks[i, s][:], func=ACT.Gelu_apprx_tanh)

        def gelu(i):
            for s in range(S_BANKS):
                gelu_bank(i, s)

        def pick_inlet(i, tag):
            scaled[i] = keep.tile([P, PAIRS], F32, name="scaled", tag=tag, align_bytes=64)
            for m0 in (0, HALF):
                cols = slice(m0, m0 + HALF)
                nc.vector.tensor_tensor(
                    out=scaled[i][:, cols],
                    in0=act[i][:].indirect(entries(pos1_sb, m0, HALF)),
                    in1=inlet_wide[:, i, cols],
                    op=ALU.mult,
                )

        def pick_outlet(i, tag):
            diff[i] = keep.tile([P, PAIRS], F32, name="diff", tag=tag, align_bytes=64)
            for m0 in (0, HALF):
                cols = slice(m0, m0 + HALF)
                nc.vector.tensor_tensor(
                    out=diff[i][:, cols],
                    in0=act[i][:].indirect(entries(pos2_sb, m0, HALF)),
                    in1=scaled[i][:, cols],
                    op=ALU.subtract,
                )

        def pick_pairs(i, tag):
            pick_inlet(i, tag)
            pick_outlet(i, "diff%d" % (i % ACT_BUFS))

        def apply_gain(i, dst, cols):
            nc.scalar.activation(out=dst[:, cols], in_=diff[i][:, cols], func=ACT.Copy, scale=neg_gain[:, i : i + 1])

        on_scalar, on_vector = nc.scalar.copy, nc.vector.tensor_copy
        every_pair = slice(0, PAIRS)


        gather_table(0, 1, "v0")
        nc.vector.tensor_copy(out=v_sc[:], in_=tab_sc[:].indirect(offs_sb[:]))
        round_w1(0, 2, on_scalar, bf_tile("bf02")[:, 0])
        quantize_w1(0, 2)
        gather_table(1, 1, "v1")
        for a in range(2):
            round_w1(0, a, on_scalar, bf_tile("bf0%d" % a)[:, 0])
            quantize_w1(0, a)
            pair_pass(0, a)
        gather_table(2, S_BANKS, "bf01")
        for s in range(S_BANKS):
            for i in range(2):
                first_product(i, 2, s)
                gelu_bank(i, s)


        both = bf_tile("tab2", 2)
        for a in range(2):
            round_w1(1, a, on_vector, both[:, a])
        for a in range(2):
            quantize_w1(1, a)
            pair_pass(1, a)
        pick_pairs(0, "ring")
        round_w1(1, 2, on_scalar, bf_tile("codes02")[:, 0])
        quantize_w1(1, 2)
        pair_pass(1, 2)
        pick_pairs(1, "codes02")
        round_w1(2, 0, on_scalar, bf_tile("sc02")[:, 0])
        quantize_w1(2, 0)
        gelu(2)
        pick_pairs(2, "sc02")
        round_w1(2, 1, on_scalar, bf_tile("codes02")[:, 0])
        round_w1(3, 0, on_scalar, bf_tile("ring")[:, 0])
        quantize_w1(2, 1)
        round_w1(2, 2, on_vector, bf_tile("sc02")[:, 0])
        quantize_w1(3, 0)
        quantize_w1(2, 2)
        gelu(3)
        pick_pairs(3, "sc02")

        z_rows = keep.tile([P, PACK, PAIRS], BF16, name="z_rows", tag="z_rows")

        def gain_and_move(u, tag):
            staged = keep.tile([P, 2, PAIRS], BF16, name="staged", tag=tag, align_bytes=64)
            for h in range(2):
                apply_gain(2 * u + h, staged[:, h], every_pair)
                for e in range(2):
                    nc.sync.dma_start(
                        out=z_rows[HALF_P * u : HALF_P * (u + 1), 2 * h + e, :],
                        in_=staged[HALF_P * e : HALF_P * (e + 1), h, :],
                    )

        gain_and_move(0, "codes12")
        round_w1(3, 1, on_scalar, bf_tile("codes02")[:, 0])
        quantize_w1(3, 1)


        pair_by_tile(2)

        z_codes = [keep.tile([P, PAIRS], U32, name="z_codes%d" % b, align_bytes=64) for b in range(H_PASSES)]
        z_sc = [keep.tile([P, PAIRS], U8, name="z_sc%d" % b, align_bytes=64) for b in range(H_PASSES)]

        def quantize_z(b, z_bf, cols):
            nc.vector.quantize_mx(
                out=z_codes[b][:, cols].bitcast(FP8X4),
                scales=z_sc[b][:, cols],
                in_=z_bf[:, cols, :].rearrange("p m t -> p (m t)"),
            )

        gelu(4)
        pick_pairs(4, "codes02")
        round_w1(3, 2, on_scalar, bf_tile("sc22")[:, 0])
        quantize_w1(3, 2)
        pair_by_tile(3)
        gelu(5)
        pick_pairs(5, "sc22")
        gain_and_move(1, "codes22")
        gelu(6)
        pick_pairs(6, "ring")
        gelu(7)
        pick_inlet(7, "sc02")
        z_bf0 = keep.tile([P, PAIRS, PACK], BF16, name="z_bf0", tag="codes32", align_bytes=64)
        nc.scalar.copy(
            out=z_bf0[:].rearrange("p (c i) t -> p c t i", i=RUN),
            in_=z_rows[:].rearrange("p t (c i) -> p c t i", i=RUN),
        )
        quantize_z(0, z_bf0, every_pair)
        pick_outlet(7, "codes32")

        z_pairs = keep.tile([P, 2, PAIRS, 2], BF16, name="z_pairs", tag="z_rows")
        for t in range(PACK - 1):
            apply_gain(PACK + t, z_pairs[:, t // 2, :, t % 2], every_pair)
        z_bf1 = keep.tile([P, PAIRS, PACK], BF16, name="z_bf1", align_bytes=64)
        halves = [slice(m0, m0 + HALF) for m0 in (0, HALF)]
        for cols in halves:
            apply_gain(TILES - 1, z_pairs[:, 1, :, 1], cols)
        words_in = z_pairs[:].rearrange("p h m e -> p h (m e)").bitcast(I32)
        words_out = z_bf1[:].bitcast(I32)
        for cols in halves:
            nc.vector.tensor_copy(
                out=words_out[:, cols, :].rearrange("p (c i) h -> p c h i", i=RUN),
                in_=words_in[:, :, cols].rearrange("p h (c i) -> p c h i", i=RUN),
            )
        for cols in halves:
            quantize_z(1, z_bf1, cols)


        for i in range(N_TILES):
            bank = psum.tile([P, BANK], F32, name="bank", tag="bank%d" % i)
            for b in range(H_PASSES):
                nc.tensor.matmul_mx(
                    out=bank[:],
                    lhsT=w4_codes[:, b, 2 * i * P : 2 * (i + 1) * P].bitcast(FP4X4),
                    lhsT_scale=w4_sc[:, b, i * P : (i + 1) * P],
                    rhs=z_codes[b][:].bitcast(FP8X4),
                    rhs_scale=z_sc[b][:],
                    start=(b == 0),
                    stop=(b == H_PASSES - 1),
                )
            y = keep.tile([P, PAIRS], F32, name="y", tag="y", bufs=N_TILES)
            nc.scalar.activation(out=y[:], in_=bank[:], func=ACT.Sin)
            left = keep.tile([P, OUT_COLS], F32, name="left", tag="left", bufs=2)
            res = keep.tile([P, OUT_COLS], F32, name="res", tag="res", bufs=N_TILES)
            for j0 in (0, OUT_HALF):
                cols = slice(j0, j0 + OUT_HALF)
                nc.vector.tensor_copy(out=left[:, cols], in_=y[:].indirect(entries(pos3_sb, j0, OUT_HALF)))
            for j0 in (0, OUT_HALF):
                cols = slice(j0, j0 + OUT_HALF)
                nc.vector.tensor_tensor(
                    out=res[:, cols], in0=y[:].indirect(entries(pos4_sb, j0, OUT_HALF)), in1=left[:, cols], op=ALU.mult
                )
            nc.sync.dma_start(out=out[i * P : (i + 1) * P, :], in_=res[:])
